import numpy as np
import ml_dtypes


def mxq(x, axis, fmt="e4m3"):
    dtype, down = {"e4m3": (ml_dtypes.float8_e4m3fn, 7), "e5m2": (ml_dtypes.float8_e5m2, 14)}[fmt]
    v = np.moveaxis(np.asarray(x, np.float32).astype(ml_dtypes.bfloat16).astype(np.float64), axis, -1)
    blocks = v.reshape(v.shape[:-1] + (-1, 32))
    amax = np.abs(blocks).max(-1, keepdims=True)
    byte = np.maximum(np.where(amax > 0, np.frexp(amax)[1] - 1 + 127, 0) - down, 1)
    scale = np.exp2(byte - 127.0)
    codes = (blocks / scale).astype(np.float32).astype(dtype).astype(np.float64)
    return np.moveaxis((codes * scale).reshape(v.shape), -1, axis)


WIDE = False


def mx_kscale(k):
    if not WIDE:
        return np.ones(k)
    levels = np.array([10, -10, 5, -5, 0])
    if k % 512:
        return np.exp2(np.random.permutation(np.resize(levels, k // 32))).repeat(32)
    a = np.empty((k // 512, 16))
    for p in range(k // 512):
        a[p, :8] = np.random.permutation(np.resize(levels, 8))
        for g in range(8):
            far = levels[np.abs(levels - a[p, g]) >= 10]
            a[p, g + 8] = far[np.random.randint(len(far))]
    return np.exp2(a.ravel()).repeat(32)


def f64(x):
    return np.asarray(x).astype(np.float64)


def striped(idx):
    return np.tile(idx.reshape(-1, 16).T, (8, 1)).astype(np.uint16)


def unstriped(offs):
    return offs[:16].T.reshape(-1).astype(np.int64)


E2M1 = np.array([0.0, 0.5, 1.0, 1.5, 2.0, 3.0, 4.0, 6.0, -0.0, -0.5, -1.0, -1.5, -2.0, -3.0, -4.0, -6.0])


def pack_weight(w, fmt):
    k, n = w.shape
    w = f64(np.asarray(w, np.float32).astype(ml_dtypes.bfloat16)).reshape(k // 32, 32, n)
    amax = np.abs(w).max(1)
    if fmt == "e4m3":
        byte = np.frexp(amax)[1] - 1 + 127 - 7
    else:
        mant, ex = np.frexp(amax / 6.0)
        byte = np.where(mant > 0.5, ex, ex - 1) + 127
    byte = np.clip(np.where(amax > 0, byte, 1), 1, 254)
    scaled = (w * np.exp2(127.0 - byte)[:, None, :]).reshape(k, n).astype(np.float32)
    by_word = np.ascontiguousarray(scaled.reshape(k // 512, 128, 4, n).transpose(0, 1, 3, 2))
    if fmt == "e4m3":
        words = by_word.astype(ml_dtypes.float8_e4m3fn).view(np.uint8)
    else:
        c = by_word.astype(ml_dtypes.float4_e2m1fn).view(np.uint8) & 0xF
        words = (c[..., 0::2] | (c[..., 1::2] << 4)).reshape(k // 512, 128, 2 * n)
    return np.ascontiguousarray(words), np.ascontiguousarray(byte.astype(np.uint8).reshape(k // 512, 16, n))


def unpack_weight(words, scales, fmt):
    g, _, n = scales.shape
    words = np.ascontiguousarray(words).reshape(g, 128, n, -1)
    if fmt == "e4m3":
        vals = words.view(ml_dtypes.float8_e4m3fn).astype(np.float64)
    else:
        nib = np.empty((g, 128, n, 4), np.uint8)
        nib[..., 0::2] = words & 0xF
        nib[..., 1::2] = words >> 4
        vals = E2M1[nib]
    vals = vals * np.repeat(np.exp2(scales.astype(np.float64) - 127.0), 8, axis=1)[..., None]
    return vals.transpose(0, 1, 3, 2).reshape(g * 512, n)


def gelu(v):
    return 0.5 * v * (1.0 + np.tanh(np.sqrt(2.0 / np.pi) * (v + 0.044715 * v**3)))


def often(T, S):
    return np.random.permutation(T)[(T * np.random.uniform(0, 1, S) ** 4).astype(np.int64)]


def bf(x):
    return np.asarray(x, np.float32).astype(ml_dtypes.bfloat16)


def planes(Y):
    n, m = Y.shape
    b = f64(bf(Y)).reshape(n // 32, 32, m)
    amax = np.abs(b).max(1)
    byte = np.clip(np.where(amax > 0, np.frexp(amax)[1] - 1 + 127 - 7, 1), 1, 254)
    codes = (b * np.exp2(127.0 - byte)[:, None, :]).reshape(n, m).astype(np.float32).astype(ml_dtypes.float8_e4m3fn).view(np.uint8)
    words = codes.reshape(n // 512, 128, 4, m).transpose(0, 1, 3, 2)
    return np.ascontiguousarray(words), np.ascontiguousarray(byte.astype(np.uint8).reshape(n // 512, 16, m))


K, T, S, H, P, N = 1024, 2048, 1024, 512, 512, 1024

def setup_inputs():
    n = np.random.standard_normal
    s = mx_kscale(K)[:, None]
    u = mx_kscale(H)[:, None]
    d = {}
    d["tab_words"], d["tab_scales"] = pack_weight(n((K, T)) * s, "e4m3")
    d["tab2_words"], d["tab2_scales"] = pack_weight(n((K, T)) * s, "e4m3")
    d["tab3_words"], d["tab3_scales"] = pack_weight(n((K, T)) * s, "e4m3")
    d["offs"] = striped(np.random.permutation(T)[:S])
    d["offs2"] = striped(np.random.permutation(T)[:S])
    d["offs3"] = striped(np.random.permutation(T)[:S])
    d["pos1"] = striped(np.random.permutation(S)[:P])
    d["pos2"] = striped(often(S, P))
    d["pos3"] = striped(often(S, P))
    d["w1"] = (n((K, H)) / s / K ** 0.5).astype(np.float32)
    d["w2_words"], d["w2_scales"] = pack_weight(0.7 * n((K, H)) / s * u.T / K ** 0.5, "e2m1")
    d["w3_words"], d["w3_scales"] = pack_weight(1.4 * n((K, H)) / s * u.T / K ** 0.5, "e4m3")
    d["rb"] = ((1.0 + 0.5 * n(H)) * u[:, 0]).astype(np.float32)
    d["w4"] = (0.5 * n((H, N)) / u / H ** 0.5 * np.exp(0.8 * n(N))[None, :]).astype(np.float32)
    return d

def reference(tab_words, tab_scales, tab2_words, tab2_scales, tab3_words, tab3_scales,
              offs, offs2, offs3, pos1, pos2, pos3, w1, w2_words, w2_scales, w3_words, w3_scales, rb, w4):
    v = unpack_weight(tab_words, tab_scales, "e4m3")[:, unstriped(offs)]
    v2 = unpack_weight(tab2_words, tab2_scales, "e4m3")[:, unstriped(offs2)]
    v3 = unpack_weight(tab3_words, tab3_scales, "e4m3")[:, unstriped(offs3)]
    a = mxq(f64(w1), 0, "e4m3").T @ v
    b = (unpack_weight(w2_words, w2_scales, "e2m1").T @ v2) + f64(rb)[:, None]
    d = unpack_weight(w3_words, w3_scales, "e4m3").T @ v3
    aj = a[:, unstriped(pos1)]
    z = aj * np.abs(aj) * b[:, unstriped(pos2)] - d[:, unstriped(pos3)]
    y = mxq(f64(w4), 0, "e4m3").T @ mxq(z, 0, "e4m3")
    words, scales = planes(y)
    return y, words, scales

@@ -1,0 +1,343 @@
+from contextlib import ExitStack
+
+import concourse.mybir as mybir
+
+K, T, S, H, M, N = 1024, 2048, 1024, 512, 512, 1024
+FLOPS = 2 * (3 * K * H * S + H * N * M)
+
+F32 = mybir.dt.float32
+BF16 = mybir.dt.bfloat16
+I32 = mybir.dt.int32
+U32 = mybir.dt.uint32
+U16 = mybir.dt.uint16
+U8 = mybir.dt.uint8
+FP8X4 = mybir.dt.float8_e4m3fn_x4
+FP4X4 = mybir.dt.float4_e2m1fn_x4
+ACT = mybir.ActivationFunctionType
+ALU = mybir.AluOpType
+
+P = 128
+PACK = 4
+PASSES = K // (P * PACK)
+BANK = 512
+CHUNK = 128
+ROWS_AT = 96
+
+
+def tile_list_colliery_regulator_join_kernel(
+    tc, tab_words, tab_scales, tab2_words, tab2_scales, tab3_words, tab3_scales,
+    offs, offs2, offs3, pos1, pos2, pos3, w1, w2_words, w2_scales, w3_words, w3_scales, rb, w4,
+    out_0, out_1, out_2,
+):
+    nc = tc.nc
+    with ExitStack() as ctx:
+        lists = ctx.enter_context(tc.tile_pool(name="lists", bufs=1))
+        keep = ctx.enter_context(tc.tile_pool(name="keep", bufs=1))
+        ring = ctx.enter_context(tc.tile_pool(name="ring", bufs=4))
+        psum = ctx.enter_context(tc.psum_pool(name="psum", bufs=4))
+
+        def load_list(src, name):
+            tile = lists.tile(list(src.shape), U16, name=name)
+            nc.sync.dma_start(tile[:], src)
+            return tile
+
+        def load_scale_rows(scales, dst):
+            nc.sync.dma_start(dst.bitcast(I32), scales.rearrange("a s n -> s a n").bitcast(I32))
+
+        def move_scale_rows(rows, plane):
+            for quad in range(4):
+                nc.gpsimd.dma_start(
+                    plane[32 * quad : 32 * quad + 4, :].bitcast(I32).rearrange("p (a n) -> p a n", a=PASSES),
+                    rows[ROWS_AT + 8 * quad : ROWS_AT + 8 * quad + 8, :].bitcast(I32),
+                )
+
+        def load_table(words, name):
+            tiles = []
+            for a in range(PASSES):
+                tile = keep.tile([P, T], U32, name="%s_words%d" % (name, a), tag="%s_words%d" % (name, a), align_bytes=64)
+                nc.sync.dma_start(tile[:].bitcast(I32), words[a].rearrange("p t i -> p (t i)").bitcast(I32))
+                tiles.append(tile)
+            return tiles
+
+        names = ("a", "b", "d")
+        table_scales = dict(zip(names, (tab_scales, tab2_scales, tab3_scales)))
+        table_lists = dict(zip(names, (offs, offs2, offs3)))
+
+        idx, scale_win, planes = {}, {}, {}
+        for x in names:
+            idx[x] = load_list(table_lists[x], "idx_" + x)
+            scale_win[x] = keep.tile([P, T], U8, name="scale_win_" + x)
+            load_scale_rows(table_scales[x], scale_win[x][ROWS_AT:P, :])
+            nc.vector.memset(scale_win[x][0:ROWS_AT, :].bitcast(I32), 0)
+        for x in names:
+            planes[x] = keep.tile([P, PASSES * S], U8, name="plane_" + x, align_bytes=64)
+            nc.vector.memset(planes[x][:].bitcast(I32), 0)
+        w_rows = keep.tile([P, 2 * PASSES * H], U8)
+        nc.vector.memset(w_rows[:].bitcast(I32), 0)
+
+        def load_weight_scales(scales, w):
+            for quad in range(4):
+                nc.sync.dma_start(
+                    w_rows[32 * quad : 32 * quad + 4, w * PASSES * H : (w + 1) * PASSES * H]
+                    .bitcast(I32)
+                    .rearrange("p (a n) -> p a n", a=PASSES),
+                    scales[:, 4 * quad : 4 * quad + 4, :].rearrange("a r n -> r a n").bitcast(I32),
+                )
+
+        def deal_weight_scales(w, name):
+            plane = keep.tile([P, PASSES * H], U8, name=name, align_bytes=64)
+            nc.vector.tensor_copy(
+                plane[:].bitcast(I32).rearrange("p (a t g) -> p a t g", a=PASSES, t=PACK),
+                w_rows[:, w * PASSES * H : (w + 1) * PASSES * H]
+                .bitcast(I32)
+                .rearrange("p (a g t) -> p a t g", a=PASSES, t=PACK),
+            )
+            return plane
+
+        w1_raw = keep.tile([P, PASSES * PACK * H], F32)
+        for a in range(PASSES):
+            nc.sync.dma_start(
+                w1_raw[:, a * PACK * H : (a + 1) * PACK * H],
+                w1[a * P * PACK : (a + 1) * P * PACK, :].rearrange("(p j) c -> p (j c)", j=PACK),
+            )
+        words_a = load_table(tab_words, "a")
+        load_weight_scales(w2_scales, 0)
+        words_b = load_table(tab2_words, "b")
+        w2_raw = keep.tile([P, PASSES * H // 2], I32)
+        nc.sync.dma_start(
+            w2_raw[:].rearrange("p (a c) -> p a c", a=PASSES), w2_words.rearrange("a p c -> p a c").bitcast(I32)
+        )
+        bias = keep.tile([P, PACK], F32)
+        with nc.allow_non_contiguous_dma(reason="one bias value for each partition and slice"):
+            for i in range(4):
+                nc.gpsimd.dma_start(bias[i:P:4, :], rb.rearrange("(g t i) -> i g t", t=PACK, i=4)[i])
+        p1 = load_list(pos1, "p1")
+        w4_raw = keep.tile([P, PACK * N], F32)
+        for t in range(PACK):
+            nc.sync.dma_start(
+                w4_raw[:, t * N : (t + 1) * N], w4.rearrange("(g t i) n -> t g i n", t=PACK, i=4)[t]
+            )
+        w3_raw = keep.tile([P, PASSES * H], I32)
+        nc.sync.dma_start(
+            w3_raw[:].rearrange("p (a c) -> p a c", a=PASSES),
+            w3_words.rearrange("a p c i -> p a (c i)").bitcast(I32),
+        )
+        words_d = load_table(tab3_words, "d")
+        load_weight_scales(w3_scales, 1)
+        p2 = load_list(pos2, "p2")
+        p3 = load_list(pos3, "p3")
+
+        for x in names:
+            picked = keep.tile([P, S], U8, name="picked_scales_" + x)
+            nc.vector.tensor_copy(picked[:], scale_win[x][:].indirect(idx[x][:]))
+            move_scale_rows(picked, planes[x])
+
+
+        def gather_table(tiles, x, slots):
+            picked = []
+            for a in range(PASSES):
+                tile = keep.tile([P, S], U32, name="picked_%s%d" % (x, a), tag=slots[a], align_bytes=64)
+                nc.vector.tensor_copy(tile[:], tiles[a][:].indirect(idx[x][:]))
+                picked.append(tile)
+            return picked
+
+        def first_stage(x, picked, stationary, drain, slots):
+            windows = []
+            for t in range(PACK):
+                window = keep.tile([P, S], F32, name="window_%s%d" % (x, t), tag=slots[t], align_bytes=64)
+                for half in range(S // BANK):
+                    cols = slice(half * BANK, (half + 1) * BANK)
+                    acc = psum.tile([P, BANK], F32, name="acc")
+                    for a in range(PASSES):
+                        codes, scales = stationary(a, t)
+                        nc.tensor.matmul_mx(
+                            out=acc[:],
+                            lhsT=codes,
+                            lhsT_scale=scales,
+                            rhs=picked[a][:, cols].bitcast(FP8X4),
+                            rhs_scale=planes[x][:, a * S + half * BANK : a * S + (half + 1) * BANK],
+                            start=(a == 0),
+                            stop=(a == PASSES - 1),
+                        )
+                    drain(window[:, cols], acc[:], t)
+                windows.append(window)
+            return windows
+
+        w1_bf = [keep.tile([P, PACK * H], BF16, tag="w1_bf%d" % a, name="w1_bf%d" % a, align_bytes=64) for a in range(PASSES)]
+        w1_codes = keep.tile([P, PASSES * H], U32, align_bytes=64)
+        w1_plane = keep.tile([P, PASSES * H], U8, align_bytes=64)
+        for a in range(PASSES):
+            part = slice(a * PACK * H, (a + 1) * PACK * H)
+            nc.scalar.copy(
+                w1_bf[a][:].rearrange("p (t g i j) -> p t g j i", t=PACK, i=4, j=PACK),
+                w1_raw[:, part].rearrange("p (j g t i) -> p t g j i", t=PACK, i=4, j=PACK),
+            )
+        picked_a = gather_table(words_a, "a", ["picked_a0", "picked_a1"])
+        for a in range(PASSES):
+            nc.vector.quantize_mx(
+                out=w1_codes[:, a * H : (a + 1) * H].bitcast(FP8X4),
+                scales=w1_plane[:, a * H : (a + 1) * H],
+                in_=w1_bf[a][:],
+            )
+
+        def w1_slice(a, t):
+            cols = slice(a * H + t * P, a * H + (t + 1) * P)
+            return w1_codes[:, cols].bitcast(FP8X4), w1_plane[:, cols]
+
+        win_a = first_stage("a", picked_a, w1_slice, lambda dst, acc, t: nc.scalar.copy(dst, acc), ["window_a%d" % t for t in range(PACK)])
+
+
+        w2_dealt = keep.tile([P, PASSES * 2 * H], U8, align_bytes=64)
+        nc.vector.tensor_copy(
+            w2_dealt[:].bitcast(I32).rearrange("p (a t g e) -> p a g t e", a=PASSES, t=PACK, e=2),
+            w2_raw[:].rearrange("p (a g t e) -> p a g t e", a=PASSES, t=PACK, e=2),
+        )
+        w2_plane = deal_weight_scales(0, "w2_plane")
+        picked_b = gather_table(words_b, "b", ["w1_bf0", "w1_bf1"])
+
+        def w2_slice(a, t):
+            at = a * 2 * H + t * 2 * P
+            return w2_dealt[:, at : at + 2 * P].bitcast(FP4X4), w2_plane[:, a * H + t * P : a * H + (t + 1) * P]
+
+        win_b = first_stage(
+            "b", picked_b, w2_slice,
+            lambda dst, acc, t: nc.scalar.activation(dst, acc, ACT.Identity, bias=bias[:, t : t + 1]),
+            ["window_b%d" % t for t in range(PACK)],
+        )
+
+        a_picked = keep.tile([P, PACK * M], F32)
+        a_abs = keep.tile([P, PACK * M], F32)
+        for t in range(PACK):
+            cols = slice(t * M, (t + 1) * M)
+            nc.vector.tensor_copy(a_picked[:, cols], win_a[t][:].indirect(p1[:]))
+            nc.scalar.activation(a_abs[:, cols], a_picked[:, cols], ACT.Abs)
+
+        w4_bf = keep.tile([P, PACK * N], BF16, align_bytes=64)
+        w4_codes = keep.tile([P, N], U32, align_bytes=64)
+        w4_plane = keep.tile([P, N], U8, align_bytes=64)
+        groups = N // (P * PACK)
+        for g in range(groups):
+            nc.scalar.copy(
+                w4_bf[:, g * PACK * BANK : (g + 1) * PACK * BANK].rearrange("p (t q j) -> p q j t", t=PACK, j=PACK),
+                w4_raw[:].rearrange("p (j g q t) -> p g q j t", j=PACK, g=groups, t=PACK)[:, g],
+            )
+            nc.vector.quantize_mx(
+                out=w4_codes[:, g * BANK : (g + 1) * BANK].bitcast(FP8X4),
+                scales=w4_plane[:, g * BANK : (g + 1) * BANK],
+                in_=w4_bf[:, g * PACK * BANK : (g + 1) * PACK * BANK],
+            )
+
+        w3_dealt = keep.tile([P, PASSES * H], U32, align_bytes=64)
+        nc.vector.tensor_copy(
+            w3_dealt[:].bitcast(I32).rearrange("p (a t g i) -> p a g t i", a=PASSES, t=PACK, i=4),
+            w3_raw[:].rearrange("p (a g t i) -> p a g t i", a=PASSES, t=PACK, i=4),
+        )
+        w3_plane = deal_weight_scales(1, "w3_plane")
+        picked_d = gather_table(words_d, "d", ["window_a3", "window_a2"])
+
+        def w3_slice(a, t):
+            cols = slice(a * H + t * P, a * H + (t + 1) * P)
+            return w3_dealt[:, cols].bitcast(FP8X4), w3_plane[:, cols]
+
+        win_d = first_stage(
+            "d", picked_d, w3_slice,
+            lambda dst, acc, t: nc.scalar.activation(dst, acc, ACT.Copy, scale=-1.0),
+            ["a_words0", "a_words1", "b_words0", "b_words1"],
+        )
+
+        a_square = keep.tile([P, PACK * M], F32, name="a_square", tag="d_words1", align_bytes=64)
+        nc.vector.tensor_tensor(a_square[:], a_abs[:], a_picked[:], ALU.mult)
+
+        z_codes = keep.tile([P, M], U32, align_bytes=64)
+        z_plane = keep.tile([P, M], U8, align_bytes=64)
+        y_codes = keep.tile([P, groups * M], U32, align_bytes=64)
+        y_plane = keep.tile([P, groups * M], U8, align_bytes=64)
+        y_rows = out_0.rearrange("(g p t) m -> g p t m", p=P, t=PACK)
+        y_words = out_1.rearrange("g p m t -> p g (m t)").bitcast(I32)
+        chunks = M // CHUNK
+
+        def offsets(pos, c):
+            return pos[:, c * CHUNK // 16 : (c + 1) * CHUNK // 16]
+
+        def gather_b(c):
+            product = []
+            for t in range(PACK):
+                tile = keep.tile([P, CHUNK], F32, name="product%d_%d" % (c, t), tag="product%d" % t, align_bytes=64)
+                nc.vector.tensor_tensor(
+                    tile[:],
+                    win_b[t][:].indirect(offsets(p2, c)),
+                    a_square[:, t * M + c * CHUNK : t * M + (c + 1) * CHUNK],
+                    ALU.mult,
+                )
+                product.append(tile)
+            return product
+
+        def gather_d(c, product):
+            z = keep.tile([P, PACK * CHUNK], F32, name="z%d" % c, tag="z_slot%d" % (c % 2), align_bytes=64)
+            for t in range(PACK):
+                nc.vector.tensor_tensor(
+                    z[:, t * CHUNK : (t + 1) * CHUNK], win_d[t][:].indirect(offsets(p3, c)), product[t][:], ALU.add
+                )
+            return z
+
+        def round_z(c, z):
+            z_bf = keep.tile([P, PACK * CHUNK], BF16, name="z_bf%d" % c, tag="z_slot%d" % ((c + 1) % 2), align_bytes=64)
+            copy = nc.vector.tensor_copy if c == chunks - 1 else nc.scalar.copy
+            copy(
+                z_bf[:].rearrange("p (c i t) -> p c t i", i=4, t=PACK),
+                z[:].rearrange("p (t c i) -> p c t i", i=4, t=PACK),
+            )
+            return z_bf
+
+        def last_product(c, z_bf):
+            chunk = slice(c * CHUNK, (c + 1) * CHUNK)
+            nc.vector.quantize_mx(out=z_codes[:, chunk].bitcast(FP8X4), scales=z_plane[:, chunk], in_=z_bf[:])
+            banks = []
+            for g in range(groups):
+                acc = psum.tile([P, BANK], F32, name="acc_y")
+                for t in range(PACK):
+                    cols = slice(g * BANK + t * P, g * BANK + (t + 1) * P)
+                    nc.tensor.matmul_mx(
+                        out=acc[:, t * CHUNK : (t + 1) * CHUNK],
+                        lhsT=w4_codes[:, cols].bitcast(FP8X4),
+                        lhsT_scale=w4_plane[:, cols],
+                        rhs=z_codes[:, chunk].bitcast(FP8X4),
+                        rhs_scale=z_plane[:, chunk],
+                        start=True,
+                        stop=True,
+                    )
+                banks.append(acc)
+            return banks
+
+        def finish(c, banks):
+            chunk = slice(c * CHUNK, (c + 1) * CHUNK)
+            copies = [nc.scalar.copy, nc.vector.tensor_copy if c == chunks - 1 else nc.scalar.copy]
+            for g in range(groups):
+                y_bf = keep.tile([P, PACK * CHUNK], BF16, name="y_bf%d_%d" % (c, g), tag="product%d" % g, align_bytes=64)
+                copies[g](
+                    y_bf[:].rearrange("p (m t) -> p m t", t=PACK), banks[g][:].rearrange("p (t m) -> p m t", t=PACK)
+                )
+                cols = slice(g * M + c * CHUNK, g * M + (c + 1) * CHUNK)
+                nc.vector.quantize_mx(out=y_codes[:, cols].bitcast(FP8X4), scales=y_plane[:, cols], in_=y_bf[:])
+            nc.sync.dma_start(
+                y_words[:, :, chunk], y_codes[:].bitcast(I32).rearrange("p (g m) -> p g m", g=groups)[:, :, chunk]
+            )
+            for g in range(groups):
+                y = ring.tile([P, PACK * CHUNK], F32, name="y")
+                copies[g](y[:], banks[g][:])
+                nc.sync.dma_start(y_rows[g][:, :, chunk], y[:].rearrange("p (t m) -> p t m", t=PACK))
+
+        z_bf = round_z(0, gather_d(0, gather_b(0)))
+        for c in range(chunks):
+            last = c == chunks - 1
+            product = None if last else gather_b(c + 1)
+            banks = last_product(c, z_bf)
+            z = None if last else gather_d(c + 1, product)
+            finish(c, banks)
+            z_bf = None if last else round_z(c + 1, z)
+        for quad in range(4):
+            queue = nc.sync if quad % 2 == 0 else nc.scalar
+            queue.dma_start(
+                out_2[:, 4 * quad : 4 * quad + 4, :].rearrange("g r m -> r g m").bitcast(I32),
+                y_plane[32 * quad : 32 * quad + 4, :].bitcast(I32).rearrange("p (g m) -> p g m", g=groups),
+            )

@@ -34,7 +34,7 @@ def tile_list_colliery_regulator_join_kernel(
         lists = ctx.enter_context(tc.tile_pool(name="lists", bufs=1))
         keep = ctx.enter_context(tc.tile_pool(name="keep", bufs=1))
         ring = ctx.enter_context(tc.tile_pool(name="ring", bufs=4))
-        psum = ctx.enter_context(tc.psum_pool(name="psum", bufs=4))
+        psum = ctx.enter_context(tc.psum_pool(name="psum", bufs=8))
 
         def load_list(src, name):
             tile = lists.tile(list(src.shape), U16, name=name)
@@ -44,109 +44,133 @@ def tile_list_colliery_regulator_join_kernel(
         def load_scale_rows(scales, dst):
             nc.sync.dma_start(dst.bitcast(I32), scales.rearrange("a s n -> s a n").bitcast(I32))
 
-        def move_scale_rows(rows, plane):
-            for quad in range(4):
-                nc.gpsimd.dma_start(
-                    plane[32 * quad : 32 * quad + 4, :].bitcast(I32).rearrange("p (a n) -> p a n", a=PASSES),
-                    rows[ROWS_AT + 8 * quad : ROWS_AT + 8 * quad + 8, :].bitcast(I32),
-                )
+        def load_words(words, x, a):
+            tile = keep.tile([P, T], U32, name="%s_words%d" % (x, a), tag="%s_words%d" % (x, a), align_bytes=64)
+            nc.sync.dma_start(tile[:].bitcast(I32), words[a].rearrange("p t i -> p (t i)").bitcast(I32))
+            return tile
 
-        def load_table(words, name):
-            tiles = []
-            for a in range(PASSES):
-                tile = keep.tile([P, T], U32, name="%s_words%d" % (name, a), tag="%s_words%d" % (name, a), align_bytes=64)
-                nc.sync.dma_start(tile[:].bitcast(I32), words[a].rearrange("p t i -> p (t i)").bitcast(I32))
-                tiles.append(tile)
-            return tiles
-
-        names = ("a", "b", "d")
-        table_scales = dict(zip(names, (tab_scales, tab2_scales, tab3_scales)))
-        table_lists = dict(zip(names, (offs, offs2, offs3)))
-
-        idx, scale_win, planes = {}, {}, {}
-        for x in names:
-            idx[x] = load_list(table_lists[x], "idx_" + x)
-            scale_win[x] = keep.tile([P, T], U8, name="scale_win_" + x)
-            load_scale_rows(table_scales[x], scale_win[x][ROWS_AT:P, :])
-            nc.vector.memset(scale_win[x][0:ROWS_AT, :].bitcast(I32), 0)
-        for x in names:
-            planes[x] = keep.tile([P, PASSES * S], U8, name="plane_" + x, align_bytes=64)
-            nc.vector.memset(planes[x][:].bitcast(I32), 0)
-        w_rows = keep.tile([P, 2 * PASSES * H], U8)
-        nc.vector.memset(w_rows[:].bitcast(I32), 0)
-
-        def load_weight_scales(scales, w):
+        def load_packed_scales(scales, window):
             for quad in range(4):
                 nc.sync.dma_start(
-                    w_rows[32 * quad : 32 * quad + 4, w * PASSES * H : (w + 1) * PASSES * H]
-                    .bitcast(I32)
-                    .rearrange("p (a n) -> p a n", a=PASSES),
+                    window[32 * quad : 32 * quad + 4 * PASSES, :].bitcast(I32),
+                    scales[:, 4 * quad : 4 * quad + 4, :].bitcast(I32),
+                )
+
+        def quad_rows(tile, quad):
+            return tile[32 * quad : 32 * quad + 4, :].bitcast(I32).rearrange("p (a n) -> p a n", a=PASSES)
+
+        def load_weight_scales(scales, rows, quads):
+            for quad in quads:
+                nc.sync.dma_start(
+                    quad_rows(rows, quad),
                     scales[:, 4 * quad : 4 * quad + 4, :].rearrange("a r n -> r a n").bitcast(I32),
                 )
 
-        def deal_weight_scales(w, name):
-            plane = keep.tile([P, PASSES * H], U8, name=name, align_bytes=64)
-            nc.vector.tensor_copy(
-                plane[:].bitcast(I32).rearrange("p (a t g) -> p a t g", a=PASSES, t=PACK),
-                w_rows[:, w * PASSES * H : (w + 1) * PASSES * H]
-                .bitcast(I32)
-                .rearrange("p (a g t) -> p a t g", a=PASSES, t=PACK),
-            )
-            return plane
+        def move_b_scales(quads):
+            for quad in quads:
+                nc.sync.dma_start(
+                    quad_rows(plane_b, quad),
+                    picked_rows_b[ROWS_AT + 8 * quad : ROWS_AT + 8 * quad + 8, :].bitcast(I32),
+                )
 
-        w1_raw = keep.tile([P, PASSES * PACK * H], F32)
-        for a in range(PASSES):
+        def load_w1(a):
+            tile = keep.tile([P, PACK * H], F32, name="w1_raw%d" % a)
             nc.sync.dma_start(
-                w1_raw[:, a * PACK * H : (a + 1) * PACK * H],
-                w1[a * P * PACK : (a + 1) * P * PACK, :].rearrange("(p j) c -> p (j c)", j=PACK),
+                tile[:], w1[a * P * PACK : (a + 1) * P * PACK, :].rearrange("(p j) c -> p (j c)", j=PACK)
             )
-        words_a = load_table(tab_words, "a")
-        load_weight_scales(w2_scales, 0)
-        words_b = load_table(tab2_words, "b")
-        w2_raw = keep.tile([P, PASSES * H // 2], I32)
-        nc.sync.dma_start(
-            w2_raw[:].rearrange("p (a c) -> p a c", a=PASSES), w2_words.rearrange("a p c -> p a c").bitcast(I32)
-        )
+            return tile
+
+        def load_w4(g):
+            tile = keep.tile([P, PACK * BANK], F32, name="w4_raw%d" % g)
+            rows = w4[:, g * BANK : (g + 1) * BANK].rearrange("(g t i) n -> t g i n", t=PACK, i=4)
+            for t in range(PACK):
+                nc.sync.dma_start(tile[:, t * BANK : (t + 1) * BANK], rows[t])
+            return tile
+
+        scale_win = {x: keep.tile([P, T], U8, name="scale_win_" + x) for x in "abd"}
+        plane_b = keep.tile([P, PASSES * S], U8, align_bytes=64)
+        w2_rows = keep.tile([P, PASSES * H], U8)
+        w3_rows = keep.tile([P, PASSES * H], U8)
+        nc.vector.memset(scale_win["a"][:].bitcast(I32), 0)
+        nc.vector.memset(scale_win["b"][0:ROWS_AT, :].bitcast(I32), 0)
+        nc.vector.memset(scale_win["d"][:].bitcast(I32), 0)
+        nc.vector.memset(plane_b[:].bitcast(I32), 0)
+        nc.vector.memset(w2_rows[:].bitcast(I32), 0)
+        nc.vector.memset(w3_rows[:].bitcast(I32), 0)
+
         bias = keep.tile([P, PACK], F32)
         with nc.allow_non_contiguous_dma(reason="one bias value for each partition and slice"):
             for i in range(4):
                 nc.gpsimd.dma_start(bias[i:P:4, :], rb.rearrange("(g t i) -> i g t", t=PACK, i=4)[i])
-        p1 = load_list(pos1, "p1")
-        w4_raw = keep.tile([P, PACK * N], F32)
-        for t in range(PACK):
-            nc.sync.dma_start(
-                w4_raw[:, t * N : (t + 1) * N], w4.rearrange("(g t i) n -> t g i n", t=PACK, i=4)[t]
-            )
+
+        idx = {}
+        idx["b"] = load_list(offs2, "idx_b")
+        load_scale_rows(tab2_scales, scale_win["b"][ROWS_AT:P, :])
+        idx["a"] = load_list(offs, "idx_a")
+        w1_raw = [load_w1(0)]
+        load_packed_scales(tab_scales, scale_win["a"])
+        words_a = [load_words(tab_words, "a", 0)]
+        idx["d"] = load_list(offs3, "idx_d")
+        w1_raw.append(load_w1(1))
+        load_packed_scales(tab3_scales, scale_win["d"])
+        words_a.append(load_words(tab_words, "a", 1))
+
+        def gather_scales(x):
+            picked = keep.tile([P, S], U8, name="picked_scales_" + x, align_bytes=64)
+            nc.vector.tensor_copy(picked[:], scale_win[x][:].indirect(idx[x][:]))
+            return picked
+
+        picked_rows_b = gather_scales("b")
+
+        load_weight_scales(w2_scales, w2_rows, (0, 1))
+        w4_raw = [load_w4(0)]
+        w2_raw = keep.tile([P, PASSES * H // 2], I32)
+        nc.sync.dma_start(
+            w2_raw[:].rearrange("p (a c) -> p a c", a=PASSES), w2_words.rearrange("a p c -> p a c").bitcast(I32)
+        )
         w3_raw = keep.tile([P, PASSES * H], I32)
         nc.sync.dma_start(
             w3_raw[:].rearrange("p (a c) -> p a c", a=PASSES),
             w3_words.rearrange("a p c i -> p a (c i)").bitcast(I32),
         )
-        words_d = load_table(tab3_words, "d")
-        load_weight_scales(w3_scales, 1)
+        load_weight_scales(w2_scales, w2_rows, (2, 3))
+        words_b = [load_words(tab2_words, "b", 0)]
+        move_b_scales((0, 1))
+        words_b.append(load_words(tab2_words, "b", 1))
+        move_b_scales((2, 3))
+        p1 = load_list(pos1, "p1")
+        w4_raw.append(load_w4(1))
+        words_d = [load_words(tab3_words, "d", 0)]
+        load_weight_scales(w3_scales, w3_rows, (0, 1, 2))
+        words_d.append(load_words(tab3_words, "d", 1))
+        load_weight_scales(w3_scales, w3_rows, (3,))
         p2 = load_list(pos2, "p2")
         p3 = load_list(pos3, "p3")
 
-        for x in names:
-            picked = keep.tile([P, S], U8, name="picked_scales_" + x)
-            nc.vector.tensor_copy(picked[:], scale_win[x][:].indirect(idx[x][:]))
-            move_scale_rows(picked, planes[x])
+        def gather_words(x, words, a, slot, pieces):
+            tile = keep.tile([P, S], U32, name="picked_%s%d" % (x, a), tag=slot, align_bytes=64)
+            width = S // pieces
+            for at in range(0, S, width):
+                nc.vector.tensor_copy(
+                    tile[:, at : at + width], words[a][:].indirect(idx[x][:, at // 16 : (at + width) // 16])
+                )
+            return tile
 
+        def deal_weight_scales(rows, name):
+            plane = keep.tile([P, PASSES * H], U8, name=name, align_bytes=64)
+            nc.vector.tensor_copy(
+                plane[:].bitcast(I32).rearrange("p (a t g) -> p a g t", a=PASSES, t=PACK),
+                rows[:].bitcast(I32).rearrange("p (a g t) -> p a g t", a=PASSES, t=PACK),
+            )
+            return plane
 
-        def gather_table(tiles, x, slots):
-            picked = []
-            for a in range(PASSES):
-                tile = keep.tile([P, S], U32, name="picked_%s%d" % (x, a), tag=slots[a], align_bytes=64)
-                nc.vector.tensor_copy(tile[:], tiles[a][:].indirect(idx[x][:]))
-                picked.append(tile)
-            return picked
-
-        def first_stage(x, picked, stationary, drain, slots):
-            windows = []
-            for t in range(PACK):
-                window = keep.tile([P, S], F32, name="window_%s%d" % (x, t), tag=slots[t], align_bytes=64)
-                for half in range(S // BANK):
-                    cols = slice(half * BANK, (half + 1) * BANK)
+        def first_stage(x, picked, moving_scales, stationary, drain, slots):
+            windows = [
+                keep.tile([P, S], F32, name="window_%s%d" % (x, t), tag=slots[t], align_bytes=64) for t in range(PACK)
+            ]
+            for half in range(S // BANK):
+                cols = slice(half * BANK, (half + 1) * BANK)
+                for t in range(PACK):
                     acc = psum.tile([P, BANK], F32, name="acc")
                     for a in range(PASSES):
                         codes, scales = stationary(a, t)
@@ -155,98 +179,104 @@ def tile_list_colliery_regulator_join_kernel(
                             lhsT=codes,
                             lhsT_scale=scales,
                             rhs=picked[a][:, cols].bitcast(FP8X4),
-                            rhs_scale=planes[x][:, a * S + half * BANK : a * S + (half + 1) * BANK],
+                            rhs_scale=moving_scales(a, cols),
                             start=(a == 0),
                             stop=(a == PASSES - 1),
                         )
-                    drain(window[:, cols], acc[:], t)
-                windows.append(window)
+                    drain(windows[t][:, cols], acc[:], t)
             return windows
 
-        w1_bf = [keep.tile([P, PACK * H], BF16, tag="w1_bf%d" % a, name="w1_bf%d" % a, align_bytes=64) for a in range(PASSES)]
+        groups = N // (P * PACK)
+        w4_bf = keep.tile([P, PACK * N], BF16, align_bytes=64)
+
+        def round_w4(g):
+            nc.scalar.copy(
+                w4_bf[:, g * PACK * BANK : (g + 1) * PACK * BANK].rearrange("p (t q j) -> p q j t", t=PACK, j=PACK),
+                w4_raw[g][:].rearrange("p (j q t) -> p q j t", j=PACK, t=PACK),
+            )
+
+        w1_bf = [
+            keep.tile([P, PACK * H], BF16, tag="w1_bf%d" % a, name="w1_bf%d" % a, align_bytes=64)
+            for a in range(PASSES)
+        ]
         w1_codes = keep.tile([P, PASSES * H], U32, align_bytes=64)
         w1_plane = keep.tile([P, PASSES * H], U8, align_bytes=64)
         for a in range(PASSES):
-            part = slice(a * PACK * H, (a + 1) * PACK * H)
             nc.scalar.copy(
                 w1_bf[a][:].rearrange("p (t g i j) -> p t g j i", t=PACK, i=4, j=PACK),
-                w1_raw[:, part].rearrange("p (j g t i) -> p t g j i", t=PACK, i=4, j=PACK),
+                w1_raw[a][:].rearrange("p (j g t i) -> p t g j i", t=PACK, i=4, j=PACK),
             )
-        picked_a = gather_table(words_a, "a", ["picked_a0", "picked_a1"])
+        round_w4(0)
+        plane_a = gather_scales("a")
+        picked_a = [gather_words("a", words_a, 0, "picked_a0", 1)]
+        plane_d = gather_scales("d")
         for a in range(PASSES):
             nc.vector.quantize_mx(
                 out=w1_codes[:, a * H : (a + 1) * H].bitcast(FP8X4),
                 scales=w1_plane[:, a * H : (a + 1) * H],
                 in_=w1_bf[a][:],
             )
+        picked_a.append(gather_words("a", words_a, 1, "w1_bf1", 1))
 
         def w1_slice(a, t):
             cols = slice(a * H + t * P, a * H + (t + 1) * P)
             return w1_codes[:, cols].bitcast(FP8X4), w1_plane[:, cols]
 
-        win_a = first_stage("a", picked_a, w1_slice, lambda dst, acc, t: nc.scalar.copy(dst, acc), ["window_a%d" % t for t in range(PACK)])
-
+        win_a = first_stage(
+            "a", picked_a, lambda a, cols: plane_a[4 * a : P, cols], w1_slice,
+            lambda dst, acc, t: nc.scalar.copy(dst, acc),
+            ["window_a%d" % t for t in range(PACK)],
+        )
 
         w2_dealt = keep.tile([P, PASSES * 2 * H], U8, align_bytes=64)
         nc.vector.tensor_copy(
             w2_dealt[:].bitcast(I32).rearrange("p (a t g e) -> p a g t e", a=PASSES, t=PACK, e=2),
             w2_raw[:].rearrange("p (a g t e) -> p a g t e", a=PASSES, t=PACK, e=2),
         )
-        w2_plane = deal_weight_scales(0, "w2_plane")
-        picked_b = gather_table(words_b, "b", ["w1_bf0", "w1_bf1"])
+        w3_dealt = keep.tile([P, PASSES * H], U32, align_bytes=64)
+        nc.vector.tensor_copy(
+            w3_dealt[:].bitcast(I32).rearrange("p (a t g i) -> p a g t i", a=PASSES, t=PACK, i=4),
+            w3_raw[:].rearrange("p (a g t i) -> p a g t i", a=PASSES, t=PACK, i=4),
+        )
+        w2_plane = deal_weight_scales(w2_rows, "w2_plane")
+        picked_b = [gather_words("b", words_b, 0, "w1_bf0", 1), gather_words("b", words_b, 1, "picked_b1", 1)]
 
         def w2_slice(a, t):
             at = a * 2 * H + t * 2 * P
             return w2_dealt[:, at : at + 2 * P].bitcast(FP4X4), w2_plane[:, a * H + t * P : a * H + (t + 1) * P]
 
         win_b = first_stage(
-            "b", picked_b, w2_slice,
+            "b", picked_b, lambda a, cols: plane_b[:, a * S + cols.start : a * S + cols.stop], w2_slice,
             lambda dst, acc, t: nc.scalar.activation(dst, acc, ACT.Identity, bias=bias[:, t : t + 1]),
             ["window_b%d" % t for t in range(PACK)],
         )
+        round_w4(1)
 
-        a_picked = keep.tile([P, PACK * M], F32)
-        a_abs = keep.tile([P, PACK * M], F32)
+        a_picked = keep.tile([P, PACK * M], F32, tag="b_words1", align_bytes=64)
         for t in range(PACK):
-            cols = slice(t * M, (t + 1) * M)
-            nc.vector.tensor_copy(a_picked[:, cols], win_a[t][:].indirect(p1[:]))
-            nc.scalar.activation(a_abs[:, cols], a_picked[:, cols], ACT.Abs)
+            nc.vector.tensor_copy(a_picked[:, t * M : (t + 1) * M], win_a[t][:].indirect(p1[:]))
+        a_abs = keep.tile([P, PACK * M], F32, tag="picked_b1", align_bytes=64)
+        nc.scalar.activation(a_abs[:], a_picked[:], ACT.Abs)
 
-        w4_bf = keep.tile([P, PACK * N], BF16, align_bytes=64)
-        w4_codes = keep.tile([P, N], U32, align_bytes=64)
-        w4_plane = keep.tile([P, N], U8, align_bytes=64)
-        groups = N // (P * PACK)
-        for g in range(groups):
-            nc.scalar.copy(
-                w4_bf[:, g * PACK * BANK : (g + 1) * PACK * BANK].rearrange("p (t q j) -> p q j t", t=PACK, j=PACK),
-                w4_raw[:].rearrange("p (j g q t) -> p g q j t", j=PACK, g=groups, t=PACK)[:, g],
-            )
-            nc.vector.quantize_mx(
-                out=w4_codes[:, g * BANK : (g + 1) * BANK].bitcast(FP8X4),
-                scales=w4_plane[:, g * BANK : (g + 1) * BANK],
-                in_=w4_bf[:, g * PACK * BANK : (g + 1) * PACK * BANK],
-            )
-
-        w3_dealt = keep.tile([P, PASSES * H], U32, align_bytes=64)
-        nc.vector.tensor_copy(
-            w3_dealt[:].bitcast(I32).rearrange("p (a t g i) -> p a g t i", a=PASSES, t=PACK, i=4),
-            w3_raw[:].rearrange("p (a g t i) -> p a g t i", a=PASSES, t=PACK, i=4),
-        )
-        w3_plane = deal_weight_scales(1, "w3_plane")
-        picked_d = gather_table(words_d, "d", ["window_a3", "window_a2"])
+        w3_plane = deal_weight_scales(w3_rows, "w3_plane")
+        picked_d = [gather_words("d", words_d, 0, "window_a3", 1), gather_words("d", words_d, 1, "window_a2", 2)]
 
         def w3_slice(a, t):
             cols = slice(a * H + t * P, a * H + (t + 1) * P)
             return w3_dealt[:, cols].bitcast(FP8X4), w3_plane[:, cols]
 
         win_d = first_stage(
-            "d", picked_d, w3_slice,
+            "d", picked_d, lambda a, cols: plane_d[4 * a : P, cols], w3_slice,
             lambda dst, acc, t: nc.scalar.activation(dst, acc, ACT.Copy, scale=-1.0),
-            ["a_words0", "a_words1", "b_words0", "b_words1"],
+            ["window_a0", "window_a1", "a_words0", "a_words1"],
         )
 
         a_square = keep.tile([P, PACK * M], F32, name="a_square", tag="d_words1", align_bytes=64)
         nc.vector.tensor_tensor(a_square[:], a_abs[:], a_picked[:], ALU.mult)
+
+        w4_codes = keep.tile([P, N], U32, tag="picked_b1", align_bytes=64)
+        w4_plane = keep.tile([P, N], U8, align_bytes=64)
+        nc.vector.quantize_mx(out=w4_codes[:].bitcast(FP8X4), scales=w4_plane[:], in_=w4_bf[:])
 
         z_codes = keep.tile([P, M], U32, align_bytes=64)
         z_plane = keep.tile([P, M], U8, align_bytes=64)
@@ -294,7 +324,7 @@ def tile_list_colliery_regulator_join_kernel(
             nc.vector.quantize_mx(out=z_codes[:, chunk].bitcast(FP8X4), scales=z_plane[:, chunk], in_=z_bf[:])
             banks = []
             for g in range(groups):
-                acc = psum.tile([P, BANK], F32, name="acc_y")
+                acc = psum.tile([P, BANK], F32, name="acc")
                 for t in range(PACK):
                     cols = slice(g * BANK + t * P, g * BANK + (t + 1) * P)
                     nc.tensor.matmul_mx(

@@ -49,13 +49,6 @@ def tile_list_colliery_regulator_join_kernel(
             nc.sync.dma_start(tile[:].bitcast(I32), words[a].rearrange("p t i -> p (t i)").bitcast(I32))
             return tile
 
-        def load_packed_scales(scales, window):
-            for quad in range(4):
-                nc.sync.dma_start(
-                    window[32 * quad : 32 * quad + 4 * PASSES, :].bitcast(I32),
-                    scales[:, 4 * quad : 4 * quad + 4, :].bitcast(I32),
-                )
-
         def quad_rows(tile, quad):
             return tile[32 * quad : 32 * quad + 4, :].bitcast(I32).rearrange("p (a n) -> p a n", a=PASSES)
 
@@ -66,11 +59,11 @@ def tile_list_colliery_regulator_join_kernel(
                     scales[:, 4 * quad : 4 * quad + 4, :].rearrange("a r n -> r a n").bitcast(I32),
                 )
 
-        def move_b_scales(quads):
+        def move_scales(x, quads):
             for quad in quads:
                 nc.sync.dma_start(
-                    quad_rows(plane_b, quad),
-                    picked_rows_b[ROWS_AT + 8 * quad : ROWS_AT + 8 * quad + 8, :].bitcast(I32),
+                    quad_rows(plane[x], quad),
+                    picked_rows[x][ROWS_AT + 8 * quad : ROWS_AT + 8 * quad + 8, :].bitcast(I32),
                 )
 
         def load_w1(a):
@@ -87,63 +80,56 @@ def tile_list_colliery_regulator_join_kernel(
                 nc.sync.dma_start(tile[:, t * BANK : (t + 1) * BANK], rows[t])
             return tile
 
-        scale_win = {x: keep.tile([P, T], U8, name="scale_win_" + x) for x in "abd"}
-        plane_b = keep.tile([P, PASSES * S], U8, align_bytes=64)
-        w2_rows = keep.tile([P, PASSES * H], U8)
-        w3_rows = keep.tile([P, PASSES * H], U8)
-        nc.vector.memset(scale_win["a"][:].bitcast(I32), 0)
-        nc.vector.memset(scale_win["b"][0:ROWS_AT, :].bitcast(I32), 0)
-        nc.vector.memset(scale_win["d"][:].bitcast(I32), 0)
-        nc.vector.memset(plane_b[:].bitcast(I32), 0)
-        nc.vector.memset(w2_rows[:].bitcast(I32), 0)
-        nc.vector.memset(w3_rows[:].bitcast(I32), 0)
-
         bias = keep.tile([P, PACK], F32)
-        with nc.allow_non_contiguous_dma(reason="one bias value for each partition and slice"):
-            for i in range(4):
-                nc.gpsimd.dma_start(bias[i:P:4, :], rb.rearrange("(g t i) -> i g t", t=PACK, i=4)[i])
 
-        idx = {}
-        idx["b"] = load_list(offs2, "idx_b")
-        load_scale_rows(tab2_scales, scale_win["b"][ROWS_AT:P, :])
-        idx["a"] = load_list(offs, "idx_a")
+        def load_bias(residues):
+            with nc.allow_non_contiguous_dma(reason="one bias value for each partition and slice"):
+                for i in residues:
+                    nc.sync.dma_start(bias[i:P:4, :], rb.rearrange("(g t i) -> i g t", t=PACK, i=4)[i])
+
+        scale_win = {x: keep.tile([P, T], U8, name="scale_win_" + x) for x in "abd"}
+        plane = {x: keep.tile([P, PASSES * S], U8, name="plane_" + x, align_bytes=64) for x in "abd"}
+        w2_rows = keep.tile([P, PASSES * H], U8)
+        w3_rows = keep.tile([P, PASSES * H], U8, tag="w3_rows", align_bytes=64)
+        for x in "abd":
+            nc.vector.memset(scale_win[x][0:ROWS_AT, :].bitcast(I32), 0)
+        for tile in (plane["a"], w2_rows, plane["b"], w3_rows, plane["d"]):
+            nc.vector.memset(tile[:].bitcast(I32), 0)
+
+        idx, picked_rows = {}, {}
+        for x, offsets, scales in (("a", offs, tab_scales), ("b", offs2, tab2_scales), ("d", offs3, tab3_scales)):
+            idx[x] = load_list(offsets, "idx_" + x)
+            load_scale_rows(scales, scale_win[x][ROWS_AT:P, :])
+            picked_rows[x] = keep.tile([P, S], U8, name="picked_rows_" + x)
+            nc.vector.tensor_copy(picked_rows[x][:], scale_win[x][:].indirect(idx[x][:]))
+
         w1_raw = [load_w1(0)]
-        load_packed_scales(tab_scales, scale_win["a"])
         words_a = [load_words(tab_words, "a", 0)]
-        idx["d"] = load_list(offs3, "idx_d")
         w1_raw.append(load_w1(1))
-        load_packed_scales(tab3_scales, scale_win["d"])
         words_a.append(load_words(tab_words, "a", 1))
-
-        def gather_scales(x):
-            picked = keep.tile([P, S], U8, name="picked_scales_" + x, align_bytes=64)
-            nc.vector.tensor_copy(picked[:], scale_win[x][:].indirect(idx[x][:]))
-            return picked
-
-        picked_rows_b = gather_scales("b")
-
-        load_weight_scales(w2_scales, w2_rows, (0, 1))
-        w4_raw = [load_w4(0)]
+        move_scales("a", (0, 2, 1, 3))
         w2_raw = keep.tile([P, PASSES * H // 2], I32)
         nc.sync.dma_start(
             w2_raw[:].rearrange("p (a c) -> p a c", a=PASSES), w2_words.rearrange("a p c -> p a c").bitcast(I32)
         )
+        words_b = [load_words(tab2_words, "b", 0)]
+        load_weight_scales(w2_scales, w2_rows, (0, 2, 1, 3))
+        words_b.append(load_words(tab2_words, "b", 1))
+        load_bias((0, 1, 2, 3))
+        move_scales("b", (0, 2))
         w3_raw = keep.tile([P, PASSES * H], I32)
         nc.sync.dma_start(
             w3_raw[:].rearrange("p (a c) -> p a c", a=PASSES),
             w3_words.rearrange("a p c i -> p a (c i)").bitcast(I32),
         )
-        load_weight_scales(w2_scales, w2_rows, (2, 3))
-        words_b = [load_words(tab2_words, "b", 0)]
-        move_b_scales((0, 1))
-        words_b.append(load_words(tab2_words, "b", 1))
-        move_b_scales((2, 3))
+        move_scales("b", (1, 3))
         p1 = load_list(pos1, "p1")
-        w4_raw.append(load_w4(1))
+        w4_raw = [load_w4(0)]
         words_d = [load_words(tab3_words, "d", 0)]
-        load_weight_scales(w3_scales, w3_rows, (0, 1, 2))
+        load_weight_scales(w3_scales, w3_rows, (0, 2, 1, 3))
         words_d.append(load_words(tab3_words, "d", 1))
-        load_weight_scales(w3_scales, w3_rows, (3,))
+        move_scales("d", (0, 2, 1, 3))
+        w4_raw.append(load_w4(1))
         p2 = load_list(pos2, "p2")
         p3 = load_list(pos3, "p3")
 
@@ -156,15 +142,15 @@ def tile_list_colliery_regulator_join_kernel(
                 )
             return tile
 
-        def deal_weight_scales(rows, name):
-            plane = keep.tile([P, PASSES * H], U8, name=name, align_bytes=64)
+        def deal_weight_scales(rows, name, slot):
+            dealt = keep.tile([P, PASSES * H], U8, name=name, tag=slot, align_bytes=64)
             nc.vector.tensor_copy(
-                plane[:].bitcast(I32).rearrange("p (a t g) -> p a g t", a=PASSES, t=PACK),
+                dealt[:].bitcast(I32).rearrange("p (a t g) -> p a g t", a=PASSES, t=PACK),
                 rows[:].bitcast(I32).rearrange("p (a g t) -> p a g t", a=PASSES, t=PACK),
             )
-            return plane
+            return dealt
 
-        def first_stage(x, picked, moving_scales, stationary, drain, slots):
+        def first_stage(x, picked, stationary, drain, slots):
             windows = [
                 keep.tile([P, S], F32, name="window_%s%d" % (x, t), tag=slots[t], align_bytes=64) for t in range(PACK)
             ]
@@ -179,7 +165,7 @@ def tile_list_colliery_regulator_join_kernel(
                             lhsT=codes,
                             lhsT_scale=scales,
                             rhs=picked[a][:, cols].bitcast(FP8X4),
-                            rhs_scale=moving_scales(a, cols),
+                            rhs_scale=plane[x][:, a * S + half * BANK : a * S + (half + 1) * BANK],
                             start=(a == 0),
                             stop=(a == PASSES - 1),
                         )
@@ -187,13 +173,18 @@ def tile_list_colliery_regulator_join_kernel(
             return windows
 
         groups = N // (P * PACK)
-        w4_bf = keep.tile([P, PACK * N], BF16, align_bytes=64)
 
-        def round_w4(g):
+        def round_w4(g, slot):
+            w4_bf = keep.tile([P, PACK * BANK], BF16, name="w4_bf%d" % g, tag=slot, align_bytes=64)
             nc.scalar.copy(
-                w4_bf[:, g * PACK * BANK : (g + 1) * PACK * BANK].rearrange("p (t q j) -> p q j t", t=PACK, j=PACK),
+                w4_bf[:].rearrange("p (t q j) -> p q j t", t=PACK, j=PACK),
                 w4_raw[g][:].rearrange("p (j q t) -> p q j t", j=PACK, t=PACK),
             )
+            return w4_bf
+
+        def quantize_w4(g, w4_bf):
+            cols = slice(g * BANK, (g + 1) * BANK)
+            nc.vector.quantize_mx(out=w4_codes[:, cols].bitcast(FP8X4), scales=w4_plane[:, cols], in_=w4_bf[:])
 
         w1_bf = [
             keep.tile([P, PACK * H], BF16, tag="w1_bf%d" % a, name="w1_bf%d" % a, align_bytes=64)
@@ -206,10 +197,7 @@ def tile_list_colliery_regulator_join_kernel(
                 w1_bf[a][:].rearrange("p (t g i j) -> p t g j i", t=PACK, i=4, j=PACK),
                 w1_raw[a][:].rearrange("p (j g t i) -> p t g j i", t=PACK, i=4, j=PACK),
             )
-        round_w4(0)
-        plane_a = gather_scales("a")
         picked_a = [gather_words("a", words_a, 0, "picked_a0", 1)]
-        plane_d = gather_scales("d")
         for a in range(PASSES):
             nc.vector.quantize_mx(
                 out=w1_codes[:, a * H : (a + 1) * H].bitcast(FP8X4),
@@ -223,7 +211,7 @@ def tile_list_colliery_regulator_join_kernel(
             return w1_codes[:, cols].bitcast(FP8X4), w1_plane[:, cols]
 
         win_a = first_stage(
-            "a", picked_a, lambda a, cols: plane_a[4 * a : P, cols], w1_slice,
+            "a", picked_a, w1_slice,
             lambda dst, acc, t: nc.scalar.copy(dst, acc),
             ["window_a%d" % t for t in range(PACK)],
         )
@@ -233,12 +221,7 @@ def tile_list_colliery_regulator_join_kernel(
             w2_dealt[:].bitcast(I32).rearrange("p (a t g e) -> p a g t e", a=PASSES, t=PACK, e=2),
             w2_raw[:].rearrange("p (a g t e) -> p a g t e", a=PASSES, t=PACK, e=2),
         )
-        w3_dealt = keep.tile([P, PASSES * H], U32, align_bytes=64)
-        nc.vector.tensor_copy(
-            w3_dealt[:].bitcast(I32).rearrange("p (a t g i) -> p a g t i", a=PASSES, t=PACK, i=4),
-            w3_raw[:].rearrange("p (a g t i) -> p a g t i", a=PASSES, t=PACK, i=4),
-        )
-        w2_plane = deal_weight_scales(w2_rows, "w2_plane")
+        w2_plane = deal_weight_scales(w2_rows, "w2_plane", "w2_plane")
         picked_b = [gather_words("b", words_b, 0, "w1_bf0", 1), gather_words("b", words_b, 1, "picked_b1", 1)]
 
         def w2_slice(a, t):
@@ -246,29 +229,34 @@ def tile_list_colliery_regulator_join_kernel(
             return w2_dealt[:, at : at + 2 * P].bitcast(FP4X4), w2_plane[:, a * H + t * P : a * H + (t + 1) * P]
 
         win_b = first_stage(
-            "b", picked_b, lambda a, cols: plane_b[:, a * S + cols.start : a * S + cols.stop], w2_slice,
+            "b", picked_b, w2_slice,
             lambda dst, acc, t: nc.scalar.activation(dst, acc, ACT.Identity, bias=bias[:, t : t + 1]),
             ["window_b%d" % t for t in range(PACK)],
         )
-        round_w4(1)
 
         a_picked = keep.tile([P, PACK * M], F32, tag="b_words1", align_bytes=64)
         for t in range(PACK):
             nc.vector.tensor_copy(a_picked[:, t * M : (t + 1) * M], win_a[t][:].indirect(p1[:]))
         a_abs = keep.tile([P, PACK * M], F32, tag="picked_b1", align_bytes=64)
         nc.scalar.activation(a_abs[:], a_picked[:], ACT.Abs)
+        w4_bf0 = round_w4(0, "window_a0")
 
-        w3_plane = deal_weight_scales(w3_rows, "w3_plane")
-        picked_d = [gather_words("d", words_d, 0, "window_a3", 1), gather_words("d", words_d, 1, "window_a2", 2)]
+        w3_dealt = keep.tile([P, PASSES * H], U32, tag="window_a1", align_bytes=64)
+        nc.vector.tensor_copy(
+            w3_dealt[:].bitcast(I32).rearrange("p (a t g i) -> p a g t i", a=PASSES, t=PACK, i=4),
+            w3_raw[:].rearrange("p (a g t i) -> p a g t i", a=PASSES, t=PACK, i=4),
+        )
+        w3_plane = deal_weight_scales(w3_rows, "w3_plane", "window_a3")
+        picked_d = [gather_words("d", words_d, 0, "window_a2", 1), gather_words("d", words_d, 1, "w3_rows", 2)]
 
         def w3_slice(a, t):
             cols = slice(a * H + t * P, a * H + (t + 1) * P)
             return w3_dealt[:, cols].bitcast(FP8X4), w3_plane[:, cols]
 
         win_d = first_stage(
-            "d", picked_d, lambda a, cols: plane_d[4 * a : P, cols], w3_slice,
+            "d", picked_d, w3_slice,
             lambda dst, acc, t: nc.scalar.activation(dst, acc, ACT.Copy, scale=-1.0),
-            ["window_a0", "window_a1", "a_words0", "a_words1"],
+            ["w1_bf0", "b_words0", "a_words0", "a_words1"],
         )
 
         a_square = keep.tile([P, PACK * M], F32, name="a_square", tag="d_words1", align_bytes=64)
@@ -276,7 +264,7 @@ def tile_list_colliery_regulator_join_kernel(
 
         w4_codes = keep.tile([P, N], U32, tag="picked_b1", align_bytes=64)
         w4_plane = keep.tile([P, N], U8, align_bytes=64)
-        nc.vector.quantize_mx(out=w4_codes[:].bitcast(FP8X4), scales=w4_plane[:], in_=w4_bf[:])
+        quantize_w4(0, w4_bf0)
 
         z_codes = keep.tile([P, M], U32, align_bytes=64)
         z_plane = keep.tile([P, M], U8, align_bytes=64)
@@ -286,27 +274,26 @@ def tile_list_colliery_regulator_join_kernel(
         y_words = out_1.rearrange("g p m t -> p g (m t)").bitcast(I32)
         chunks = M // CHUNK
 
-        def offsets(pos, c):
+        def chunk_offsets(pos, c):
             return pos[:, c * CHUNK // 16 : (c + 1) * CHUNK // 16]
 
         def gather_b(c):
-            product = []
+            product = keep.tile([P, PACK * CHUNK], F32, name="product%d" % c, tag="product")
             for t in range(PACK):
-                tile = keep.tile([P, CHUNK], F32, name="product%d_%d" % (c, t), tag="product%d" % t, align_bytes=64)
                 nc.vector.tensor_tensor(
-                    tile[:],
-                    win_b[t][:].indirect(offsets(p2, c)),
+                    product[:, t * CHUNK : (t + 1) * CHUNK],
+                    win_b[t][:].indirect(chunk_offsets(p2, c)),
                     a_square[:, t * M + c * CHUNK : t * M + (c + 1) * CHUNK],
                     ALU.mult,
                 )
-                product.append(tile)
             return product
 
         def gather_d(c, product):
             z = keep.tile([P, PACK * CHUNK], F32, name="z%d" % c, tag="z_slot%d" % (c % 2), align_bytes=64)
             for t in range(PACK):
+                cols = slice(t * CHUNK, (t + 1) * CHUNK)
                 nc.vector.tensor_tensor(
-                    z[:, t * CHUNK : (t + 1) * CHUNK], win_d[t][:].indirect(offsets(p3, c)), product[t][:], ALU.add
+                    z[:, cols], win_d[t][:].indirect(chunk_offsets(p3, c)), product[:, cols], ALU.add
                 )
             return z
 
@@ -339,12 +326,22 @@ def tile_list_colliery_regulator_join_kernel(
                 banks.append(acc)
             return banks
 
-        def finish(c, banks):
-            chunk = slice(c * CHUNK, (c + 1) * CHUNK)
-            copies = [nc.scalar.copy, nc.vector.tensor_copy if c == chunks - 1 else nc.scalar.copy]
+        def drain_engine(c, g):
+            return nc.vector.tensor_copy if (c, g) == (chunks - 1, groups - 1) else nc.scalar.copy
+
+        def store_y(c, banks):
             for g in range(groups):
-                y_bf = keep.tile([P, PACK * CHUNK], BF16, name="y_bf%d_%d" % (c, g), tag="product%d" % g, align_bytes=64)
-                copies[g](
+                y = ring.tile([P, PACK * CHUNK], F32, name="y")
+                drain_engine(c, g)(y[:], banks[g][:])
+                nc.sync.dma_start(
+                    y_rows[g][:, :, c * CHUNK : (c + 1) * CHUNK], y[:].rearrange("p (t m) -> p t m", t=PACK)
+                )
+
+        def quantize_y(c, banks):
+            chunk = slice(c * CHUNK, (c + 1) * CHUNK)
+            for g in reversed(range(groups)) if c == chunks - 1 else range(groups):
+                y_bf = ring.tile([P, PACK * CHUNK], BF16, name="y_bf", align_bytes=64)
+                drain_engine(c, g)(
                     y_bf[:].rearrange("p (m t) -> p m t", t=PACK), banks[g][:].rearrange("p (t m) -> p m t", t=PACK)
                 )
                 cols = slice(g * M + c * CHUNK, g * M + (c + 1) * CHUNK)
@@ -352,18 +349,16 @@ def tile_list_colliery_regulator_join_kernel(
             nc.sync.dma_start(
                 y_words[:, :, chunk], y_codes[:].bitcast(I32).rearrange("p (g m) -> p g m", g=groups)[:, :, chunk]
             )
-            for g in range(groups):
-                y = ring.tile([P, PACK * CHUNK], F32, name="y")
-                copies[g](y[:], banks[g][:])
-                nc.sync.dma_start(y_rows[g][:, :, chunk], y[:].rearrange("p (t m) -> p t m", t=PACK))
 
         z_bf = round_z(0, gather_d(0, gather_b(0)))
+        quantize_w4(1, round_w4(1, "z_slot0"))
         for c in range(chunks):
             last = c == chunks - 1
             product = None if last else gather_b(c + 1)
             banks = last_product(c, z_bf)
             z = None if last else gather_d(c + 1, product)
-            finish(c, banks)
+            for finish in (store_y, quantize_y) if last else (quantize_y, store_y):
+                finish(c, banks)
             z_bf = None if last else round_z(c + 1, z)
         for quad in range(4):
             queue = nc.sync if quad % 2 == 0 else nc.scalar

from contextlib import ExitStack

import concourse.mybir as mybir

K, T, S, H, M, N = 1024, 2048, 1024, 512, 512, 1024
FLOPS = 2 * (3 * K * H * S + H * N * M)

F32 = mybir.dt.float32
BF16 = mybir.dt.bfloat16
I32 = mybir.dt.int32
U32 = mybir.dt.uint32
U16 = mybir.dt.uint16
U8 = mybir.dt.uint8
FP8X4 = mybir.dt.float8_e4m3fn_x4
FP4X4 = mybir.dt.float4_e2m1fn_x4
ACT = mybir.ActivationFunctionType
ALU = mybir.AluOpType

P = 128
PACK = 4
PASSES = K // (P * PACK)
BANK = 512
CHUNK = 128
ROWS_AT = 96


def tile_list_colliery_regulator_join_kernel(
    tc, tab_words, tab_scales, tab2_words, tab2_scales, tab3_words, tab3_scales,
    offs, offs2, offs3, pos1, pos2, pos3, w1, w2_words, w2_scales, w3_words, w3_scales, rb, w4,
    out_0, out_1, out_2,
):
    nc = tc.nc
    with ExitStack() as ctx:
        lists = ctx.enter_context(tc.tile_pool(name="lists", bufs=1))
        keep = ctx.enter_context(tc.tile_pool(name="keep", bufs=1))
        ring = ctx.enter_context(tc.tile_pool(name="ring", bufs=4))
        psum = ctx.enter_context(tc.psum_pool(name="psum", bufs=8))

        def load_list(src, name):
            tile = lists.tile(list(src.shape), U16, name=name)
            nc.sync.dma_start(tile[:], src)
            return tile

        def load_scale_rows(scales, dst):
            nc.sync.dma_start(dst.bitcast(I32), scales.rearrange("a s n -> s a n").bitcast(I32))

        def load_words(words, x, a):
            tile = keep.tile([P, T], U32, name="%s_words%d" % (x, a), tag="%s_words%d" % (x, a), align_bytes=64)
            nc.sync.dma_start(tile[:].bitcast(I32), words[a].rearrange("p t i -> p (t i)").bitcast(I32))
            return tile

        def quad_rows(tile, quad):
            return tile[32 * quad : 32 * quad + 4, :].bitcast(I32).rearrange("p (a n) -> p a n", a=PASSES)

        def load_weight_scales(scales, rows, quads):
            for quad in quads:
                nc.sync.dma_start(
                    quad_rows(rows, quad),
                    scales[:, 4 * quad : 4 * quad + 4, :].rearrange("a r n -> r a n").bitcast(I32),
                )

        def move_scales(x, quads):
            for quad in quads:
                nc.sync.dma_start(
                    quad_rows(plane[x], quad),
                    picked_rows[x][ROWS_AT + 8 * quad : ROWS_AT + 8 * quad + 8, :].bitcast(I32),
                )

        def load_w1(a):
            tile = keep.tile([P, PACK * H], F32, name="w1_raw%d" % a)
            nc.sync.dma_start(
                tile[:], w1[a * P * PACK : (a + 1) * P * PACK, :].rearrange("(p j) c -> p (j c)", j=PACK)
            )
            return tile

        def load_w4(g):
            tile = keep.tile([P, PACK * BANK], F32, name="w4_raw%d" % g)
            rows = w4[:, g * BANK : (g + 1) * BANK].rearrange("(g t i) n -> t g i n", t=PACK, i=4)
            for t in range(PACK):
                nc.sync.dma_start(tile[:, t * BANK : (t + 1) * BANK], rows[t])
            return tile

        bias = keep.tile([P, PACK], F32)

        def load_bias(residues):
            with nc.allow_non_contiguous_dma(reason="one bias value for each partition and slice"):
                for i in residues:
                    nc.sync.dma_start(bias[i:P:4, :], rb.rearrange("(g t i) -> i g t", t=PACK, i=4)[i])

        scale_win = {x: keep.tile([P, T], U8, name="scale_win_" + x) for x in "abd"}
        plane = {x: keep.tile([P, PASSES * S], U8, name="plane_" + x, align_bytes=64) for x in "abd"}
        w2_rows = keep.tile([P, PASSES * H], U8)
        w3_rows = keep.tile([P, PASSES * H], U8, tag="w3_rows", align_bytes=64)
        for x in "abd":
            nc.vector.memset(scale_win[x][0:ROWS_AT, :].bitcast(I32), 0)
        for tile in (plane["a"], w2_rows, plane["b"], w3_rows, plane["d"]):
            nc.vector.memset(tile[:].bitcast(I32), 0)

        idx, picked_rows = {}, {}
        for x, offsets, scales in (("a", offs, tab_scales), ("b", offs2, tab2_scales), ("d", offs3, tab3_scales)):
            idx[x] = load_list(offsets, "idx_" + x)
            load_scale_rows(scales, scale_win[x][ROWS_AT:P, :])
            picked_rows[x] = keep.tile([P, S], U8, name="picked_rows_" + x)
            nc.vector.tensor_copy(picked_rows[x][:], scale_win[x][:].indirect(idx[x][:]))

        w1_raw = [load_w1(0)]
        words_a = [load_words(tab_words, "a", 0)]
        w1_raw.append(load_w1(1))
        words_a.append(load_words(tab_words, "a", 1))
        move_scales("a", (0, 2, 1, 3))
        w2_raw = keep.tile([P, PASSES * H // 2], I32)
        nc.sync.dma_start(
            w2_raw[:].rearrange("p (a c) -> p a c", a=PASSES), w2_words.rearrange("a p c -> p a c").bitcast(I32)
        )
        words_b = [load_words(tab2_words, "b", 0)]
        load_weight_scales(w2_scales, w2_rows, (0, 2, 1, 3))
        words_b.append(load_words(tab2_words, "b", 1))
        load_bias((0, 1, 2, 3))
        move_scales("b", (0, 2))
        w3_raw = keep.tile([P, PASSES * H], I32)
        nc.sync.dma_start(
            w3_raw[:].rearrange("p (a c) -> p a c", a=PASSES),
            w3_words.rearrange("a p c i -> p a (c i)").bitcast(I32),
        )
        move_scales("b", (1, 3))
        p1 = load_list(pos1, "p1")
        w4_raw = [load_w4(0)]
        words_d = [load_words(tab3_words, "d", 0)]
        load_weight_scales(w3_scales, w3_rows, (0, 2, 1, 3))
        words_d.append(load_words(tab3_words, "d", 1))
        move_scales("d", (0, 2, 1, 3))
        w4_raw.append(load_w4(1))
        p2 = load_list(pos2, "p2")
        p3 = load_list(pos3, "p3")

        def gather_words(x, words, a, slot, pieces):
            tile = keep.tile([P, S], U32, name="picked_%s%d" % (x, a), tag=slot, align_bytes=64)
            width = S // pieces
            for at in range(0, S, width):
                nc.vector.tensor_copy(
                    tile[:, at : at + width], words[a][:].indirect(idx[x][:, at // 16 : (at + width) // 16])
                )
            return tile

        def deal_weight_scales(rows, name, slot):
            dealt = keep.tile([P, PASSES * H], U8, name=name, tag=slot, align_bytes=64)
            nc.vector.tensor_copy(
                dealt[:].bitcast(I32).rearrange("p (a t g) -> p a g t", a=PASSES, t=PACK),
                rows[:].bitcast(I32).rearrange("p (a g t) -> p a g t", a=PASSES, t=PACK),
            )
            return dealt

        def first_stage(x, picked, stationary, drain, slots):
            windows = [
                keep.tile([P, S], F32, name="window_%s%d" % (x, t), tag=slots[t], align_bytes=64) for t in range(PACK)
            ]
            for half in range(S // BANK):
                cols = slice(half * BANK, (half + 1) * BANK)
                for t in range(PACK):
                    acc = psum.tile([P, BANK], F32, name="acc")
                    for a in range(PASSES):
                        codes, scales = stationary(a, t)
                        nc.tensor.matmul_mx(
                            out=acc[:],
                            lhsT=codes,
                            lhsT_scale=scales,
                            rhs=picked[a][:, cols].bitcast(FP8X4),
                            rhs_scale=plane[x][:, a * S + half * BANK : a * S + (half + 1) * BANK],
                            start=(a == 0),
                            stop=(a == PASSES - 1),
                        )
                    drain(windows[t][:, cols], acc[:], t)
            return windows

        groups = N // (P * PACK)

        def round_w4(g, slot):
            w4_bf = keep.tile([P, PACK * BANK], BF16, name="w4_bf%d" % g, tag=slot, align_bytes=64)
            nc.scalar.copy(
                w4_bf[:].rearrange("p (t q j) -> p q j t", t=PACK, j=PACK),
                w4_raw[g][:].rearrange("p (j q t) -> p q j t", j=PACK, t=PACK),
            )
            return w4_bf

        def quantize_w4(g, w4_bf):
            cols = slice(g * BANK, (g + 1) * BANK)
            nc.vector.quantize_mx(out=w4_codes[:, cols].bitcast(FP8X4), scales=w4_plane[:, cols], in_=w4_bf[:])

        w1_bf = [
            keep.tile([P, PACK * H], BF16, tag="w1_bf%d" % a, name="w1_bf%d" % a, align_bytes=64)
            for a in range(PASSES)
        ]
        w1_codes = keep.tile([P, PASSES * H], U32, align_bytes=64)
        w1_plane = keep.tile([P, PASSES * H], U8, align_bytes=64)
        for a in range(PASSES):
            nc.scalar.copy(
                w1_bf[a][:].rearrange("p (t g i j) -> p t g j i", t=PACK, i=4, j=PACK),
                w1_raw[a][:].rearrange("p (j g t i) -> p t g j i", t=PACK, i=4, j=PACK),
            )
        picked_a = [gather_words("a", words_a, 0, "picked_a0", 1)]
        for a in range(PASSES):
            nc.vector.quantize_mx(
                out=w1_codes[:, a * H : (a + 1) * H].bitcast(FP8X4),
                scales=w1_plane[:, a * H : (a + 1) * H],
                in_=w1_bf[a][:],
            )
        picked_a.append(gather_words("a", words_a, 1, "w1_bf1", 1))

        def w1_slice(a, t):
            cols = slice(a * H + t * P, a * H + (t + 1) * P)
            return w1_codes[:, cols].bitcast(FP8X4), w1_plane[:, cols]

        win_a = first_stage(
            "a", picked_a, w1_slice,
            lambda dst, acc, t: nc.scalar.copy(dst, acc),
            ["window_a%d" % t for t in range(PACK)],
        )

        w2_dealt = keep.tile([P, PASSES * 2 * H], U8, align_bytes=64)
        nc.vector.tensor_copy(
            w2_dealt[:].bitcast(I32).rearrange("p (a t g e) -> p a g t e", a=PASSES, t=PACK, e=2),
            w2_raw[:].rearrange("p (a g t e) -> p a g t e", a=PASSES, t=PACK, e=2),
        )
        w2_plane = deal_weight_scales(w2_rows, "w2_plane", "w2_plane")
        picked_b = [gather_words("b", words_b, 0, "w1_bf0", 1), gather_words("b", words_b, 1, "picked_b1", 1)]

        def w2_slice(a, t):
            at = a * 2 * H + t * 2 * P
            return w2_dealt[:, at : at + 2 * P].bitcast(FP4X4), w2_plane[:, a * H + t * P : a * H + (t + 1) * P]

        win_b = first_stage(
            "b", picked_b, w2_slice,
            lambda dst, acc, t: nc.scalar.activation(dst, acc, ACT.Identity, bias=bias[:, t : t + 1]),
            ["window_b%d" % t for t in range(PACK)],
        )

        a_picked = keep.tile([P, PACK * M], F32, tag="b_words1", align_bytes=64)
        for t in range(PACK):
            nc.vector.tensor_copy(a_picked[:, t * M : (t + 1) * M], win_a[t][:].indirect(p1[:]))
        a_abs = keep.tile([P, PACK * M], F32, tag="picked_b1", align_bytes=64)
        nc.scalar.activation(a_abs[:], a_picked[:], ACT.Abs)
        w4_bf0 = round_w4(0, "window_a0")

        w3_dealt = keep.tile([P, PASSES * H], U32, tag="window_a1", align_bytes=64)
        nc.vector.tensor_copy(
            w3_dealt[:].bitcast(I32).rearrange("p (a t g i) -> p a g t i", a=PASSES, t=PACK, i=4),
            w3_raw[:].rearrange("p (a g t i) -> p a g t i", a=PASSES, t=PACK, i=4),
        )
        w3_plane = deal_weight_scales(w3_rows, "w3_plane", "window_a3")
        picked_d = [gather_words("d", words_d, 0, "window_a2", 1), gather_words("d", words_d, 1, "w3_rows", 2)]

        def w3_slice(a, t):
            cols = slice(a * H + t * P, a * H + (t + 1) * P)
            return w3_dealt[:, cols].bitcast(FP8X4), w3_plane[:, cols]

        win_d = first_stage(
            "d", picked_d, w3_slice,
            lambda dst, acc, t: nc.scalar.activation(dst, acc, ACT.Copy, scale=-1.0),
            ["w1_bf0", "b_words0", "a_words0", "a_words1"],
        )

        a_square = keep.tile([P, PACK * M], F32, name="a_square", tag="d_words1", align_bytes=64)
        nc.vector.tensor_tensor(a_square[:], a_abs[:], a_picked[:], ALU.mult)

        w4_codes = keep.tile([P, N], U32, tag="picked_b1", align_bytes=64)
        w4_plane = keep.tile([P, N], U8, align_bytes=64)
        quantize_w4(0, w4_bf0)

        z_codes = keep.tile([P, M], U32, align_bytes=64)
        z_plane = keep.tile([P, M], U8, align_bytes=64)
        y_codes = keep.tile([P, groups * M], U32, align_bytes=64)
        y_plane = keep.tile([P, groups * M], U8, align_bytes=64)
        y_rows = out_0.rearrange("(g p t) m -> g p t m", p=P, t=PACK)
        y_words = out_1.rearrange("g p m t -> p g (m t)").bitcast(I32)
        chunks = M // CHUNK

        def chunk_offsets(pos, c):
            return pos[:, c * CHUNK // 16 : (c + 1) * CHUNK // 16]

        def gather_b(c):
            product = keep.tile([P, PACK * CHUNK], F32, name="product%d" % c, tag="product")
            for t in range(PACK):
                nc.vector.tensor_tensor(
                    product[:, t * CHUNK : (t + 1) * CHUNK],
                    win_b[t][:].indirect(chunk_offsets(p2, c)),
                    a_square[:, t * M + c * CHUNK : t * M + (c + 1) * CHUNK],
                    ALU.mult,
                )
            return product

        def gather_d(c, product):
            z = keep.tile([P, PACK * CHUNK], F32, name="z%d" % c, tag="z_slot%d" % (c % 2), align_bytes=64)
            for t in range(PACK):
                cols = slice(t * CHUNK, (t + 1) * CHUNK)
                nc.vector.tensor_tensor(
                    z[:, cols], win_d[t][:].indirect(chunk_offsets(p3, c)), product[:, cols], ALU.add
                )
            return z

        def round_z(c, z):
            z_bf = keep.tile([P, PACK * CHUNK], BF16, name="z_bf%d" % c, tag="z_slot%d" % ((c + 1) % 2), align_bytes=64)
            copy = nc.vector.tensor_copy if c == chunks - 1 else nc.scalar.copy
            copy(
                z_bf[:].rearrange("p (c i t) -> p c t i", i=4, t=PACK),
                z[:].rearrange("p (t c i) -> p c t i", i=4, t=PACK),
            )
            return z_bf

        def last_product(c, z_bf):
            chunk = slice(c * CHUNK, (c + 1) * CHUNK)
            nc.vector.quantize_mx(out=z_codes[:, chunk].bitcast(FP8X4), scales=z_plane[:, chunk], in_=z_bf[:])
            banks = []
            for g in range(groups):
                acc = psum.tile([P, BANK], F32, name="acc")
                for t in range(PACK):
                    cols = slice(g * BANK + t * P, g * BANK + (t + 1) * P)
                    nc.tensor.matmul_mx(
                        out=acc[:, t * CHUNK : (t + 1) * CHUNK],
                        lhsT=w4_codes[:, cols].bitcast(FP8X4),
                        lhsT_scale=w4_plane[:, cols],
                        rhs=z_codes[:, chunk].bitcast(FP8X4),
                        rhs_scale=z_plane[:, chunk],
                        start=True,
                        stop=True,
                    )
                banks.append(acc)
            return banks

        def drain_engine(c, g):
            return nc.vector.tensor_copy if (c, g) == (chunks - 1, groups - 1) else nc.scalar.copy

        def store_y(c, banks):
            for g in range(groups):
                y = ring.tile([P, PACK * CHUNK], F32, name="y")
                drain_engine(c, g)(y[:], banks[g][:])
                nc.sync.dma_start(
                    y_rows[g][:, :, c * CHUNK : (c + 1) * CHUNK], y[:].rearrange("p (t m) -> p t m", t=PACK)
                )

        def quantize_y(c, banks):
            chunk = slice(c * CHUNK, (c + 1) * CHUNK)
            for g in reversed(range(groups)) if c == chunks - 1 else range(groups):
                y_bf = ring.tile([P, PACK * CHUNK], BF16, name="y_bf", align_bytes=64)
                drain_engine(c, g)(
                    y_bf[:].rearrange("p (m t) -> p m t", t=PACK), banks[g][:].rearrange("p (t m) -> p m t", t=PACK)
                )
                cols = slice(g * M + c * CHUNK, g * M + (c + 1) * CHUNK)
                nc.vector.quantize_mx(out=y_codes[:, cols].bitcast(FP8X4), scales=y_plane[:, cols], in_=y_bf[:])
            nc.sync.dma_start(
                y_words[:, :, chunk], y_codes[:].bitcast(I32).rearrange("p (g m) -> p g m", g=groups)[:, :, chunk]
            )

        z_bf = round_z(0, gather_d(0, gather_b(0)))
        quantize_w4(1, round_w4(1, "z_slot0"))
        for c in range(chunks):
            last = c == chunks - 1
            product = None if last else gather_b(c + 1)
            banks = last_product(c, z_bf)
            z = None if last else gather_d(c + 1, product)
            for finish in (store_y, quantize_y) if last else (quantize_y, store_y):
                finish(c, banks)
            z_bf = None if last else round_z(c + 1, z)
        for quad in range(4):
            queue = nc.sync if quad % 2 == 0 else nc.scalar
            queue.dma_start(
                out_2[:, 4 * quad : 4 * quad + 4, :].rearrange("g r m -> r g m").bitcast(I32),
                y_plane[32 * quad : 32 * quad + 4, :].bitcast(I32).rearrange("p (g m) -> p g m", g=groups),
            )
